import numpy as np
import ml_dtypes


def mxq(x, axis, fmt="e4m3"):
    dtype, down = {"e4m3": (ml_dtypes.float8_e4m3fn, 7), "e5m2": (ml_dtypes.float8_e5m2, 14)}[fmt]
    v = np.moveaxis(np.asarray(x, np.float32).astype(ml_dtypes.bfloat16).astype(np.float64), axis, -1)
    blocks = v.reshape(v.shape[:-1] + (-1, 32))
    amax = np.abs(blocks).max(-1, keepdims=True)
    byte = np.maximum(np.where(amax > 0, np.frexp(amax)[1] - 1 + 127, 0) - down, 1)
    scale = np.exp2(byte - 127.0)
    codes = (blocks / scale).astype(np.float32).astype(dtype).astype(np.float64)
    return np.moveaxis((codes * scale).reshape(v.shape), -1, axis)


WIDE = False


def mx_kscale(k):
    if not WIDE:
        return np.ones(k)
    levels = np.array([30, -30])
    if k % 512:
        return np.exp2(np.random.permutation(np.resize(levels, k // 32))).repeat(32)
    a = np.empty((k // 512, 16))
    for p in range(k // 512):
        a[p, :8] = np.random.permutation(np.resize(levels, 8))
        for g in range(8):
            far = levels[np.abs(levels - a[p, g]) >= 10]
            a[p, g + 8] = far[np.random.randint(len(far))]
    return np.exp2(a.ravel()).repeat(32)


def f64(x):
    return np.asarray(x).astype(np.float64)


def striped(idx):
    return np.tile(np.asarray(idx).reshape(-1, 16).T, (8, 1)).astype(np.uint16)


def unstriped(offs):
    return offs[:16].T.reshape(-1).astype(np.int64)


E2M1 = np.array([0.0, 0.5, 1.0, 1.5, 2.0, 3.0, 4.0, 6.0, -0.0, -0.5, -1.0, -1.5, -2.0, -3.0, -4.0, -6.0])


def pack_weight(w, fmt):
    k, n = w.shape
    w = f64(np.asarray(w, np.float32).astype(ml_dtypes.bfloat16)).reshape(k // 32, 32, n)
    amax = np.abs(w).max(1)
    if fmt in ("e4m3", "e5m2"):
        byte = np.frexp(amax)[1] - 1 + 127 - (7 if fmt == "e4m3" else 14)
    else:
        mant, ex = np.frexp(amax / 6.0)
        byte = np.where(mant > 0.5, ex, ex - 1) + 127
    byte = np.clip(np.where(amax > 0, byte, 1), 1, 254)
    scaled = (w * np.exp2(127.0 - byte)[:, None, :]).reshape(k, n).astype(np.float32)
    by_word = np.ascontiguousarray(scaled.reshape(k // 512, 128, 4, n).transpose(0, 1, 3, 2))
    if fmt in ("e4m3", "e5m2"):
        words = by_word.astype(ml_dtypes.float8_e4m3fn if fmt == "e4m3" else ml_dtypes.float8_e5m2).view(np.uint8)
    else:
        c = by_word.astype(ml_dtypes.float4_e2m1fn).view(np.uint8) & 0xF
        words = (c[..., 0::2] | (c[..., 1::2] << 4)).reshape(k // 512, 128, 2 * n)
    return np.ascontiguousarray(words), np.ascontiguousarray(byte.astype(np.uint8).reshape(k // 512, 16, n))


def unpack_weight(words, scales, fmt):
    g, _, n = scales.shape
    words = np.ascontiguousarray(words).reshape(g, 128, n, -1)
    if fmt in ("e4m3", "e5m2"):
        vals = words.view(ml_dtypes.float8_e4m3fn if fmt == "e4m3" else ml_dtypes.float8_e5m2).astype(np.float64)
    else:
        nib = np.empty((g, 128, n, 4), np.uint8)
        nib[..., 0::2] = words & 0xF
        nib[..., 1::2] = words >> 4
        vals = E2M1[nib]
    vals = vals * np.repeat(np.exp2(scales.astype(np.float64) - 127.0), 8, axis=1)[..., None]
    return vals.transpose(0, 1, 3, 2).reshape(g * 512, n)


K, T, J, S, R, O, N = 512, 512, 256, 512, 512, 128, 256


def setup_inputs():
    n = np.random.standard_normal
    idx = np.random.permutation(T)[:J]
    idx2 = np.random.permutation(S)[:J]
    idx3 = np.random.permutation(J)[:O]
    idx4 = np.random.permutation(J)[:O]
    fk = mx_kscale(K)
    fr = mx_kscale(R)
    wp = pack_weight(n((K, R)) * 1 / np.sqrt(K) * fk[:, None] * fr, "e5m2")
    wbp = pack_weight(n((R, N)) * 1 / np.sqrt(R) / fr[:, None], "e4m3")
    return {
        "xa": (n((K, T))).astype(np.float32),
        "xb": (n((K, S))).astype(np.float32),
        "fk": (np.random.uniform(0.5, 2.0, (K, 1)) / fk[:, None]).astype(np.float32),
        "w_words": wp[0],
        "w_scales": wp[1],
        "wb_words": wbp[0],
        "wb_scales": wbp[1],
        "rs": (1.0 * n((O, N))).astype(np.float32),
        "offs": striped(idx),
        "offs2": striped(idx2),
        "offs3": striped(idx3),
        "offs4": striped(idx4),
    }


def reference(xa, xb, fk, w_words, w_scales, wb_words, wb_scales, rs, offs, offs2, offs3, offs4):
    idx = unstriped(offs)
    idx2 = unstriped(offs2)
    idx3 = unstriped(offs3)
    idx4 = unstriped(offs4)
    wu = unpack_weight(w_words, w_scales, "e5m2")
    wbu = unpack_weight(wb_words, wb_scales, "e4m3")
    u = f64(xa)[:, idx] * f64(xb)[:, idx2] * f64(fk)
    uq = mxq(u, 0, "e5m2")
    a = wu.T @ uq
    ha = np.maximum(a, 0.0)
    hid = ha[:, idx3] - ha[:, idx4]
    hidq = mxq(hid, 0, "e5m2")
    p = hidq.T @ wbu
    mn = np.mean(np.abs(p), axis=1, keepdims=True)
    y = np.maximum(p - mn, 0.0) - 0.3 * f64(rs)
    return y

@@ -1,0 +1,136 @@
+from contextlib import ExitStack
+
+import concourse.mybir as mybir
+
+K, T, J, S, R, O, N = 512, 512, 256, 512, 512, 128, 256
+FLOPS = 2 * K * R * J + 2 * R * O * N
+
+F32 = mybir.dt.float32
+BF16 = mybir.dt.bfloat16
+I32 = mybir.dt.int32
+U32 = mybir.dt.uint32
+U16 = mybir.dt.uint16
+U8 = mybir.dt.uint8
+E5M2X4 = mybir.dt.float8_e5m2_x4
+E4M3X4 = mybir.dt.float8_e4m3fn_x4
+ALU = mybir.AluOpType
+ACT = mybir.ActivationFunctionType
+
+P = 128
+PACK = 4
+
+
+def tile_list_looks_entryproducts_gap_rowabove_kernel(
+    tc, xa, xb, fk, w_words, w_scales, wb_words, wb_scales, rs, offs, offs2, offs3, offs4, out
+):
+    nc = tc.nc
+    with ExitStack() as ctx:
+        sb = ctx.enter_context(tc.tile_pool(name="sb", bufs=1))
+        ps = ctx.enter_context(tc.psum_pool(name="ps", bufs=1))
+
+        l1 = sb.tile([P, J // 16], U16, name="l1")
+        l2 = sb.tile([P, J // 16], U16, name="l2")
+        l3 = sb.tile([P, O // 16], U16, name="l3")
+        l4 = sb.tile([P, O // 16], U16, name="l4")
+        xa_sb = [sb.tile([P, 2 * T], F32, name="xa%d" % h) for h in range(2)]
+        xb_sb = [sb.tile([P, S], F32, name="xb%d" % t) for t in range(PACK)]
+        fk_sb = sb.tile([P, PACK], F32, name="fk_sb")
+        w_raw = sb.tile([P, R], U32, name="w_raw", align_bytes=64)
+        w_st = sb.tile([P, R], U32, name="w_st", align_bytes=64)
+        ws_raw = sb.tile([P, R], U8, name="ws_raw", align_bytes=64)
+        ws_st = sb.tile([P, R], U8, name="ws_st", align_bytes=64)
+        wb_sb = sb.tile([P, N], U32, name="wb_sb", align_bytes=64)
+        wbs = sb.tile([P, N], U8, name="wbs", align_bytes=64)
+        rs_sb = sb.tile([P, N], F32, name="rs_sb")
+
+        xa_rows = xa.rearrange("(p h t) c -> p h (t c)", h=2, t=2)
+        xb_rows = xb.rearrange("(p t) c -> p t c", t=PACK)
+
+        nc.gpsimd.memset(ws_raw[:].bitcast(I32), 0)
+        nc.gpsimd.memset(wbs[:].bitcast(I32), 0)
+
+        nc.sync.dma_start(xa_sb[0][:], xa_rows[:, 0, :])
+        nc.sync.dma_start(l1[:], offs)
+        nc.sync.dma_start(fk_sb[:], fk.rearrange("(p t) one -> p (t one)", t=PACK))
+        nc.sync.dma_start(xb_sb[0][:], xb_rows[:, 0, :])
+        nc.sync.dma_start(l2[:], offs2)
+        nc.sync.dma_start(xa_sb[1][:], xa_rows[:, 1, :])
+        nc.sync.dma_start(xb_sb[1][:], xb_rows[:, 1, :])
+        for q in range(4):
+            nc.sync.dma_start(ws_raw[32 * q : 32 * q + 4, :].bitcast(I32), w_scales[0, 4 * q : 4 * q + 4, :].bitcast(I32))
+        for t in range(2, PACK):
+            nc.sync.dma_start(xb_sb[t][:], xb_rows[:, t, :])
+        nc.sync.dma_start(w_raw[:].bitcast(I32), w_words[0].rearrange("p n t -> p (n t)").bitcast(I32))
+        nc.sync.dma_start(l3[:], offs3)
+        nc.sync.dma_start(l4[:], offs4)
+        nc.sync.dma_start(wb_sb[:].bitcast(I32), wb_words[0].rearrange("p n t -> p (n t)").bitcast(I32))
+        nc.sync.dma_start(rs_sb[:], rs)
+        for q in range(4):
+            nc.sync.dma_start(wbs[32 * q : 32 * q + 4, :].bitcast(I32), wb_scales[0, 4 * q : 4 * q + 4, :].bitcast(I32))
+
+        g1 = sb.tile([P, PACK, J], F32, name="g1")
+        ga = sb.tile([P, PACK, J], F32, name="ga")
+        prod = sb.tile([P, PACK, J], F32, name="prod")
+        for t in range(PACK):
+            win = xa_sb[t // 2][:, (t % 2) * T : (t % 2 + 1) * T]
+            nc.scalar.activation(g1[:, t, :], win.indirect(l1[:]), ACT.Copy)
+            nc.scalar.activation(ga[:, t, :], g1[:, t, :], ACT.Copy, scale=fk_sb[:, t : t + 1])
+            nc.vector.tensor_tensor(prod[:, t, :], xb_sb[t][:].indirect(l2[:]), ga[:, t, :], ALU.mult)
+            if t == 1:
+                nc.vector.tensor_copy(
+                    ws_st[:].rearrange("p (t m) -> p t m", t=PACK), ws_raw[:].rearrange("p (m t) -> p t m", t=PACK)
+                )
+
+        u_bf = sb.tile([P, J * PACK], BF16, name="u_bf", align_bytes=64)
+        nc.vector.tensor_copy(
+            u_bf[:].rearrange("p (c i t) -> p c t i", i=4, t=PACK), prod[:].rearrange("p t (c i) -> p c t i", i=4)
+        )
+        nc.vector.tensor_copy(
+            w_st[:].rearrange("p (t c i) -> p c t i", t=PACK, i=4), w_raw[:].rearrange("p (c i t) -> p c t i", i=4, t=PACK)
+        )
+        u_q = sb.tile([P, J], U32, name="u_q", align_bytes=64)
+        u_s = sb.tile([P, J], U8, name="u_s", align_bytes=64)
+        nc.vector.quantize_mx(out=u_q[:].bitcast(E5M2X4), scales=u_s[:], in_=u_bf[:])
+
+        hid = sb.tile([P, PACK, O], F32, name="hid")
+        g4 = sb.tile([P, PACK, O], F32, name="g4")
+        for t in range(PACK):
+            acc = ps.tile([P, J], F32, name="acc%d" % t)
+            cols = slice(t * P, (t + 1) * P)
+            nc.tensor.matmul_mx(
+                out=acc[:], lhsT=w_st[:, cols].bitcast(E5M2X4), lhsT_scale=ws_st[:, cols],
+                rhs=u_q[:].bitcast(E5M2X4), rhs_scale=u_s[:], start=True, stop=True,
+            )
+            ha = sb.tile([P, J], F32, name="ha%d" % t)
+            if t == 0:
+                nc.vector.tensor_scalar(ha[:], acc[:], 0.0, None, ALU.max)
+                nc.vector.tensor_copy(g4[:, t, :], ha[:].indirect(l4[:]))
+            else:
+                nc.scalar.activation(ha[:], acc[:], ACT.Relu)
+                nc.scalar.activation(g4[:, t, :], ha[:].indirect(l4[:]), ACT.Copy)
+            nc.vector.tensor_tensor(hid[:, t, :], ha[:].indirect(l3[:]), g4[:, t, :], ALU.subtract)
+
+        nres = sb.tile([P, N], F32, name="nres")
+        nc.scalar.activation(nres[:], rs_sb[:], ACT.Copy, scale=-0.3)
+
+        h_bf = sb.tile([P, O * PACK], BF16, name="h_bf", align_bytes=64)
+        nc.vector.tensor_copy(
+            h_bf[:].rearrange("p (c i t) -> p c t i", i=4, t=PACK), hid[:].rearrange("p t (c i) -> p c t i", i=4)
+        )
+        h_q = sb.tile([P, O], U32, name="h_q", align_bytes=64)
+        h_s = sb.tile([P, O], U8, name="h_s", align_bytes=64)
+        nc.vector.quantize_mx(out=h_q[:].bitcast(E5M2X4), scales=h_s[:], in_=h_bf[:])
+
+        pp = ps.tile([P, N], F32, name="pp")
+        nc.tensor.matmul_mx(
+            out=pp[:], lhsT=h_q[:].bitcast(E5M2X4), lhsT_scale=h_s[:],
+            rhs=wb_sb[:].bitcast(E4M3X4), rhs_scale=wbs[:], start=True, stop=True,
+        )
+        qq = sb.tile([P, N], F32, name="qq")
+        nc.vector.tensor_tensor(qq[:], pp[:], nres[:], ALU.add)
+        mag = sb.tile([P, N], F32, name="mag")
+        mn = sb.tile([P, 1], F32, name="mn")
+        nc.scalar.activation(mag[:], pp[:], ACT.Abs, scale=1.0 / N, accum_out=mn[:])
+        y = sb.tile([P, N], F32, name="y")
+        nc.vector.scalar_tensor_tensor(y[:], qq[:], mn[:], nres[:], ALU.subtract, ALU.max)
+        nc.sync.dma_start(out, y[:])

@@ -32,105 +32,153 @@ def tile_list_looks_entryproducts_gap_rowabove_kernel(
         l2 = sb.tile([P, J // 16], U16, name="l2")
         l3 = sb.tile([P, O // 16], U16, name="l3")
         l4 = sb.tile([P, O // 16], U16, name="l4")
-        xa_sb = [sb.tile([P, 2 * T], F32, name="xa%d" % h) for h in range(2)]
+        xa_sb = [sb.tile([P, T], F32, name="xa%d" % t) for t in range(PACK)]
         xb_sb = [sb.tile([P, S], F32, name="xb%d" % t) for t in range(PACK)]
         fk_sb = sb.tile([P, PACK], F32, name="fk_sb")
         w_raw = sb.tile([P, R], U32, name="w_raw", align_bytes=64)
         w_st = sb.tile([P, R], U32, name="w_st", align_bytes=64)
-        ws_raw = sb.tile([P, R], U8, name="ws_raw", align_bytes=64)
+        ws_raw = sb.tile([P, R], U8, name="ws_raw", tag="plane", align_bytes=64)
         ws_st = sb.tile([P, R], U8, name="ws_st", align_bytes=64)
-        wb_sb = sb.tile([P, N], U32, name="wb_sb", align_bytes=64)
-        wbs = sb.tile([P, N], U8, name="wbs", align_bytes=64)
-        rs_sb = sb.tile([P, N], F32, name="rs_sb")
 
-        xa_rows = xa.rearrange("(p h t) c -> p h (t c)", h=2, t=2)
+        xa_rows = xa.rearrange("(p t) c -> p t c", t=PACK)
         xb_rows = xb.rearrange("(p t) c -> p t c", t=PACK)
 
+        warm_in = sb.tile([P, 1], F32, name="warm_in")
+        warm_out = sb.tile([P, 1], F32, name="warm_out")
+        ws_mid = sb.tile([P, R], U8, name="ws_mid", align_bytes=64)
         nc.gpsimd.memset(ws_raw[:].bitcast(I32), 0)
-        nc.gpsimd.memset(wbs[:].bitcast(I32), 0)
+        nc.gpsimd.memset(warm_in[:], 0.0)
+        nc.scalar.activation(warm_out[:], warm_in[:], ACT.Abs)
+        nc.gpsimd.memset(ws_st[:].bitcast(I32), 0)
 
-        nc.sync.dma_start(xa_sb[0][:], xa_rows[:, 0, :])
         nc.sync.dma_start(l1[:], offs)
+        nc.sync.dma_start(xa_sb[0][:], xa_rows[:, 0, :])
+        nc.sync.dma_start(xa_sb[1][:], xa_rows[:, 1, :])
         nc.sync.dma_start(fk_sb[:], fk.rearrange("(p t) one -> p (t one)", t=PACK))
+        nc.sync.dma_start(ws_raw[0:16, :].bitcast(I32), w_scales[0].bitcast(I32))
         nc.sync.dma_start(xb_sb[0][:], xb_rows[:, 0, :])
         nc.sync.dma_start(l2[:], offs2)
-        nc.sync.dma_start(xa_sb[1][:], xa_rows[:, 1, :])
-        nc.sync.dma_start(xb_sb[1][:], xb_rows[:, 1, :])
-        for q in range(4):
-            nc.sync.dma_start(ws_raw[32 * q : 32 * q + 4, :].bitcast(I32), w_scales[0, 4 * q : 4 * q + 4, :].bitcast(I32))
-        for t in range(2, PACK):
+        nc.sync.dma_start(xa_sb[2][:], xa_rows[:, 2, :])
+        nc.sync.dma_start(xa_sb[3][:], xa_rows[:, 3, :])
+        for t in range(1, PACK):
             nc.sync.dma_start(xb_sb[t][:], xb_rows[:, t, :])
         nc.sync.dma_start(w_raw[:].bitcast(I32), w_words[0].rearrange("p n t -> p (n t)").bitcast(I32))
+        nc.vector.tensor_copy(
+            ws_mid[:].rearrange("p (t m) -> p t m", t=PACK), ws_raw[:].rearrange("p (m t) -> p t m", t=PACK)
+        )
+        for q in range(4):
+            nc.sync.dma_start(ws_st[32 * q : 32 * q + 4, :].bitcast(I32), ws_mid[4 * q : 4 * q + 4, :].bitcast(I32))
         nc.sync.dma_start(l3[:], offs3)
         nc.sync.dma_start(l4[:], offs4)
+
+        g1 = [sb.tile([P, J], F32, name="g1_%d" % t, tag="slot%d" % t, align_bytes=64) for t in range(PACK)]
+        ga = sb.tile([P, PACK, J], F32, name="ga")
+        gb = sb.tile([P, 2, J // 2], F32, name="gb")
+        prod = sb.tile([P, PACK, J], F32, name="prod")
+        H = J // 2
+
+        nc.vector.tensor_copy(g1[0][:], xa_sb[0][:].indirect(l1[:]))
+        nc.vector.tensor_scalar(ga[:, 0, :], g1[0][:], fk_sb[:, 0:1], None, ALU.mult)
+        for t in (1, 2):
+            nc.scalar.activation(g1[t][:], xa_sb[t][:].indirect(l1[:]), ACT.Copy)
+            nc.scalar.activation(ga[:, t, :], g1[t][:], ACT.Copy, scale=fk_sb[:, t : t + 1])
+        nc.vector.tensor_tensor(prod[:, 0, :], xb_sb[0][:].indirect(l2[:]), ga[:, 0, :], ALU.mult)
+        nc.vector.tensor_copy(g1[3][:], xa_sb[3][:].indirect(l1[:]))
+        nc.scalar.activation(ga[:, 3, :], g1[3][:], ACT.Copy, scale=fk_sb[:, 3:4])
+        wbs = sb.tile([P, N], U8, name="wbs", tag="plane", align_bytes=64)
+        nc.gpsimd.memset(wbs[:].bitcast(I32), 0)
+        wb_sb = sb.tile([P, N], U32, name="wb_sb", tag="slot0", align_bytes=64)
+        rs_sb = sb.tile([P, N], F32, name="rs_sb", tag="slot1", align_bytes=64)
         nc.sync.dma_start(wb_sb[:].bitcast(I32), wb_words[0].rearrange("p n t -> p (n t)").bitcast(I32))
         nc.sync.dma_start(rs_sb[:], rs)
         for q in range(4):
             nc.sync.dma_start(wbs[32 * q : 32 * q + 4, :].bitcast(I32), wb_scales[0, 4 * q : 4 * q + 4, :].bitcast(I32))
 
-        g1 = sb.tile([P, PACK, J], F32, name="g1")
-        ga = sb.tile([P, PACK, J], F32, name="ga")
-        prod = sb.tile([P, PACK, J], F32, name="prod")
-        for t in range(PACK):
-            win = xa_sb[t // 2][:, (t % 2) * T : (t % 2 + 1) * T]
-            nc.scalar.activation(g1[:, t, :], win.indirect(l1[:]), ACT.Copy)
-            nc.scalar.activation(ga[:, t, :], g1[:, t, :], ACT.Copy, scale=fk_sb[:, t : t + 1])
-            nc.vector.tensor_tensor(prod[:, t, :], xb_sb[t][:].indirect(l2[:]), ga[:, t, :], ALU.mult)
-            if t == 1:
-                nc.vector.tensor_copy(
-                    ws_st[:].rearrange("p (t m) -> p t m", t=PACK), ws_raw[:].rearrange("p (m t) -> p t m", t=PACK)
-                )
+        nc.vector.tensor_tensor(prod[:, 1, :], xb_sb[1][:].indirect(l2[:]), ga[:, 1, :], ALU.mult)
+        for t in (2, 3):
+            nc.vector.tensor_tensor(prod[:, t, 0:H], xb_sb[t][:].indirect(l2[:, 0:8]), ga[:, t, 0:H], ALU.mult)
+            nc.scalar.activation(gb[:, t - 2, :], xb_sb[t][:].indirect(l2[:, 8:16]), ACT.Copy)
+        nc.vector.tensor_tensor(prod[:, 2:4, H:J], gb[:], ga[:, 2:4, H:J], ALU.mult)
 
-        u_bf = sb.tile([P, J * PACK], BF16, name="u_bf", align_bytes=64)
-        nc.vector.tensor_copy(
-            u_bf[:].rearrange("p (c i t) -> p c t i", i=4, t=PACK), prod[:].rearrange("p t (c i) -> p c t i", i=4)
+        u_bf = [sb.tile([P, H * PACK], BF16, name="u_bf%d" % h, tag="half%d" % h, align_bytes=64) for h in range(2)]
+        nc.scalar.copy(
+            u_bf[0][:].rearrange("p (c i t) -> p c t i", i=4, t=PACK),
+            prod[:, :, 0:H].rearrange("p t (c i) -> p c t i", i=4),
         )
         nc.vector.tensor_copy(
             w_st[:].rearrange("p (t c i) -> p c t i", t=PACK, i=4), w_raw[:].rearrange("p (c i t) -> p c t i", i=4, t=PACK)
         )
+        nc.vector.tensor_copy(
+            u_bf[1][:].rearrange("p (c i t) -> p c t i", i=4, t=PACK),
+            prod[:, :, H:J].rearrange("p t (c i) -> p c t i", i=4),
+        )
         u_q = sb.tile([P, J], U32, name="u_q", align_bytes=64)
         u_s = sb.tile([P, J], U8, name="u_s", align_bytes=64)
-        nc.vector.quantize_mx(out=u_q[:].bitcast(E5M2X4), scales=u_s[:], in_=u_bf[:])
+        for h in range(2):
+            cols = slice(h * H, (h + 1) * H)
+            nc.vector.quantize_mx(out=u_q[:, cols].bitcast(E5M2X4), scales=u_s[:, cols], in_=u_bf[h][:])
 
-        hid = sb.tile([P, PACK, O], F32, name="hid")
+        g3 = sb.tile([P, PACK, O], F32, name="g3")
         g4 = sb.tile([P, PACK, O], F32, name="g4")
-        for t in range(PACK):
-            acc = ps.tile([P, J], F32, name="acc%d" % t)
+        ha = [sb.tile([P, J], F32, name="ha%d" % t) for t in range(PACK)]
+        acc = [ps.tile([P, J], F32, name="acc%d" % t) for t in range(PACK)]
+
+        def first_product(t, slots):
             cols = slice(t * P, (t + 1) * P)
             nc.tensor.matmul_mx(
-                out=acc[:], lhsT=w_st[:, cols].bitcast(E5M2X4), lhsT_scale=ws_st[:, cols],
-                rhs=u_q[:].bitcast(E5M2X4), rhs_scale=u_s[:], start=True, stop=True,
+                out=acc[t][:, slots], lhsT=w_st[:, cols].bitcast(E5M2X4), lhsT_scale=ws_st[:, cols],
+                rhs=u_q[:, slots].bitcast(E5M2X4), rhs_scale=u_s[:, slots], start=True, stop=True,
             )
-            ha = sb.tile([P, J], F32, name="ha%d" % t)
-            if t == 0:
-                nc.vector.tensor_scalar(ha[:], acc[:], 0.0, None, ALU.max)
-                nc.vector.tensor_copy(g4[:, t, :], ha[:].indirect(l4[:]))
-            else:
-                nc.scalar.activation(ha[:], acc[:], ACT.Relu)
-                nc.scalar.activation(g4[:, t, :], ha[:].indirect(l4[:]), ACT.Copy)
-            nc.vector.tensor_tensor(hid[:, t, :], ha[:].indirect(l3[:]), g4[:, t, :], ALU.subtract)
 
-        nres = sb.tile([P, N], F32, name="nres")
-        nc.scalar.activation(nres[:], rs_sb[:], ACT.Copy, scale=-0.3)
+        for h in range(2):
+            for t in range(2):
+                first_product(t, slice(h * H, (h + 1) * H))
+        for t in range(2, PACK):
+            first_product(t, slice(0, J))
+        for t in range(PACK):
+            nc.scalar.activation(ha[t][:], acc[t][:], ACT.Relu)
+        nres = sb.tile([P, N], F32, name="nres", tag="half1", align_bytes=64)
+        nc.vector.tensor_scalar(nres[:], rs_sb[:], -0.3, None, ALU.mult)
+        for t in range(PACK):
+            if t < 3:
+                nc.vector.tensor_copy(g3[:, t, :], ha[t][:].indirect(l3[:]))
+            else:
+                nc.scalar.activation(g3[:, t, :], ha[t][:].indirect(l3[:]), ACT.Copy)
+            if t < 2:
+                nc.vector.tensor_copy(g4[:, t, :], ha[t][:].indirect(l4[:]))
+            else:
+                nc.scalar.activation(g4[:, t, :], ha[t][:].indirect(l4[:]), ACT.Copy)
 
         h_bf = sb.tile([P, O * PACK], BF16, name="h_bf", align_bytes=64)
-        nc.vector.tensor_copy(
-            h_bf[:].rearrange("p (c i t) -> p c t i", i=4, t=PACK), hid[:].rearrange("p t (c i) -> p c t i", i=4)
-        )
+        for u in range(2):
+            pair = slice(2 * u, 2 * u + 2)
+            nc.vector.tensor_tensor(
+                h_bf[:].rearrange("p (c i t) -> p c t i", i=4, t=PACK)[:, :, pair, :],
+                g3[:, pair, :].rearrange("p t (c i) -> p c t i", i=4),
+                g4[:, pair, :].rearrange("p t (c i) -> p c t i", i=4),
+                ALU.subtract,
+            )
         h_q = sb.tile([P, O], U32, name="h_q", align_bytes=64)
         h_s = sb.tile([P, O], U8, name="h_s", align_bytes=64)
         nc.vector.quantize_mx(out=h_q[:].bitcast(E5M2X4), scales=h_s[:], in_=h_bf[:])
 
-        pp = ps.tile([P, N], F32, name="pp")
-        nc.tensor.matmul_mx(
-            out=pp[:], lhsT=h_q[:].bitcast(E5M2X4), lhsT_scale=h_s[:],
-            rhs=wb_sb[:].bitcast(E4M3X4), rhs_scale=wbs[:], start=True, stop=True,
-        )
-        qq = sb.tile([P, N], F32, name="qq")
-        nc.vector.tensor_tensor(qq[:], pp[:], nres[:], ALU.add)
+        NH = N // 2
+        pp = [ps.tile([P, NH], F32, name="pp%d" % h) for h in range(2)]
         mag = sb.tile([P, N], F32, name="mag")
-        mn = sb.tile([P, 1], F32, name="mn")
-        nc.scalar.activation(mag[:], pp[:], ACT.Abs, scale=1.0 / N, accum_out=mn[:])
+        mn = [sb.tile([P, 1], F32, name="mn%d" % h) for h in range(2)]
+        qq = sb.tile([P, N], F32, name="qq")
         y = sb.tile([P, N], F32, name="y")
-        nc.vector.scalar_tensor_tensor(y[:], qq[:], mn[:], nres[:], ALU.subtract, ALU.max)
+        for h in range(2):
+            cols = slice(h * NH, (h + 1) * NH)
+            nc.tensor.matmul_mx(
+                out=pp[h][:], lhsT=h_q[:].bitcast(E5M2X4), lhsT_scale=h_s[:],
+                rhs=wb_sb[:, cols].bitcast(E4M3X4), rhs_scale=wbs[:, cols], start=True, stop=True,
+            )
+            nc.scalar.activation(mag[:, cols], pp[h][:], ACT.Abs, scale=1.0 / N, accum_out=mn[h][:])
+        for h in range(2):
+            cols = slice(h * NH, (h + 1) * NH)
+            nc.vector.scalar_tensor_tensor(qq[:, cols], pp[h][:], mn[0][:], nres[:, cols], ALU.subtract, ALU.add)
+        for h in range(2):
+            cols = slice(h * NH, (h + 1) * NH)
+            nc.vector.scalar_tensor_tensor(y[:, cols], qq[:, cols], mn[1][:], nres[:, cols], ALU.subtract, ALU.max)
         nc.sync.dma_start(out, y[:])

@@ -32,75 +32,68 @@ def tile_list_looks_entryproducts_gap_rowabove_kernel(
         l2 = sb.tile([P, J // 16], U16, name="l2")
         l3 = sb.tile([P, O // 16], U16, name="l3")
         l4 = sb.tile([P, O // 16], U16, name="l4")
-        xa_sb = [sb.tile([P, T], F32, name="xa%d" % t) for t in range(PACK)]
+        xa_sb = [sb.tile([P, 2 * T], F32, name="xa%d" % u) for u in range(2)]
         xb_sb = [sb.tile([P, S], F32, name="xb%d" % t) for t in range(PACK)]
         fk_sb = sb.tile([P, PACK], F32, name="fk_sb")
         w_raw = sb.tile([P, R], U32, name="w_raw", align_bytes=64)
         w_st = sb.tile([P, R], U32, name="w_st", align_bytes=64)
-        ws_raw = sb.tile([P, R], U8, name="ws_raw", tag="plane", align_bytes=64)
-        ws_st = sb.tile([P, R], U8, name="ws_st", align_bytes=64)
+        ws_raw = sb.tile([P, R], U8, name="ws_raw", align_bytes=64)
+        ws_st = sb.tile([P, R + N], U8, name="ws_st", align_bytes=64)
 
-        xa_rows = xa.rearrange("(p t) c -> p t c", t=PACK)
+        xa_rows = xa.rearrange("(p u e) c -> p u (e c)", u=2, e=2)
         xb_rows = xb.rearrange("(p t) c -> p t c", t=PACK)
 
         warm_in = sb.tile([P, 1], F32, name="warm_in")
         warm_out = sb.tile([P, 1], F32, name="warm_out")
-        ws_mid = sb.tile([P, R], U8, name="ws_mid", align_bytes=64)
+        ws_mid = sb.tile([P, R + N], U8, name="ws_mid", align_bytes=64)
         nc.gpsimd.memset(ws_raw[:].bitcast(I32), 0)
         nc.gpsimd.memset(warm_in[:], 0.0)
         nc.scalar.activation(warm_out[:], warm_in[:], ACT.Abs)
         nc.gpsimd.memset(ws_st[:].bitcast(I32), 0)
 
         nc.sync.dma_start(l1[:], offs)
-        nc.sync.dma_start(xa_sb[0][:], xa_rows[:, 0, :])
-        nc.sync.dma_start(xa_sb[1][:], xa_rows[:, 1, :])
         nc.sync.dma_start(fk_sb[:], fk.rearrange("(p t) one -> p (t one)", t=PACK))
+        nc.sync.dma_start(xa_sb[0][:], xa_rows[:, 0, :])
+        nc.sync.dma_start(ws_mid[0:16, R : R + N].bitcast(I32), wb_scales[0].bitcast(I32))
         nc.sync.dma_start(ws_raw[0:16, :].bitcast(I32), w_scales[0].bitcast(I32))
         nc.sync.dma_start(xb_sb[0][:], xb_rows[:, 0, :])
         nc.sync.dma_start(l2[:], offs2)
-        nc.sync.dma_start(xa_sb[2][:], xa_rows[:, 2, :])
-        nc.sync.dma_start(xa_sb[3][:], xa_rows[:, 3, :])
+        nc.sync.dma_start(xa_sb[1][:], xa_rows[:, 1, :])
         for t in range(1, PACK):
             nc.sync.dma_start(xb_sb[t][:], xb_rows[:, t, :])
         nc.sync.dma_start(w_raw[:].bitcast(I32), w_words[0].rearrange("p n t -> p (n t)").bitcast(I32))
         nc.vector.tensor_copy(
-            ws_mid[:].rearrange("p (t m) -> p t m", t=PACK), ws_raw[:].rearrange("p (m t) -> p t m", t=PACK)
+            ws_mid[:, 0:R].rearrange("p (t m) -> p t m", t=PACK), ws_raw[:].rearrange("p (m t) -> p t m", t=PACK)
         )
         for q in range(4):
             nc.sync.dma_start(ws_st[32 * q : 32 * q + 4, :].bitcast(I32), ws_mid[4 * q : 4 * q + 4, :].bitcast(I32))
         nc.sync.dma_start(l3[:], offs3)
         nc.sync.dma_start(l4[:], offs4)
 
-        g1 = [sb.tile([P, J], F32, name="g1_%d" % t, tag="slot%d" % t, align_bytes=64) for t in range(PACK)]
+        g1 = [sb.tile([P, J], F32, name="g1_%d" % u, tag="slot%d" % u, align_bytes=64) for u in range(2)]
+        fk_rep = sb.tile([P, 2, J], F32, name="fk_rep")
         ga = sb.tile([P, PACK, J], F32, name="ga")
         gb = sb.tile([P, 2, J // 2], F32, name="gb")
         prod = sb.tile([P, PACK, J], F32, name="prod")
         H = J // 2
 
-        nc.vector.tensor_copy(g1[0][:], xa_sb[0][:].indirect(l1[:]))
-        nc.vector.tensor_scalar(ga[:, 0, :], g1[0][:], fk_sb[:, 0:1], None, ALU.mult)
-        for t in (1, 2):
-            nc.scalar.activation(g1[t][:], xa_sb[t][:].indirect(l1[:]), ACT.Copy)
-            nc.scalar.activation(ga[:, t, :], g1[t][:], ACT.Copy, scale=fk_sb[:, t : t + 1])
-        nc.vector.tensor_tensor(prod[:, 0, :], xb_sb[0][:].indirect(l2[:]), ga[:, 0, :], ALU.mult)
-        nc.vector.tensor_copy(g1[3][:], xa_sb[3][:].indirect(l1[:]))
-        nc.scalar.activation(ga[:, 3, :], g1[3][:], ACT.Copy, scale=fk_sb[:, 3:4])
-        wbs = sb.tile([P, N], U8, name="wbs", tag="plane", align_bytes=64)
-        nc.gpsimd.memset(wbs[:].bitcast(I32), 0)
+        nc.vector.tensor_copy(fk_rep[:], fk_sb[:, 0:PACK:2].unsqueeze(2).to_broadcast([P, 2, J]))
+        for u in range(2):
+            nc.vector.tensor_tensor(ga[:, 2 * u, :], xa_sb[u][:].indirect(l1[:]), fk_rep[:, u, :], ALU.mult)
+            nc.scalar.activation(g1[u][:], xa_sb[u][:, T : 2 * T].indirect(l1[:]), ACT.Copy)
+            nc.scalar.activation(ga[:, 2 * u + 1, :], g1[u][:], ACT.Copy, scale=fk_sb[:, 2 * u + 1 : 2 * u + 2])
+            nc.vector.tensor_tensor(prod[:, u, :], xb_sb[u][:].indirect(l2[:]), ga[:, u, :], ALU.mult)
         wb_sb = sb.tile([P, N], U32, name="wb_sb", tag="slot0", align_bytes=64)
         rs_sb = sb.tile([P, N], F32, name="rs_sb", tag="slot1", align_bytes=64)
         nc.sync.dma_start(wb_sb[:].bitcast(I32), wb_words[0].rearrange("p n t -> p (n t)").bitcast(I32))
         nc.sync.dma_start(rs_sb[:], rs)
-        for q in range(4):
-            nc.sync.dma_start(wbs[32 * q : 32 * q + 4, :].bitcast(I32), wb_scales[0, 4 * q : 4 * q + 4, :].bitcast(I32))
 
-        nc.vector.tensor_tensor(prod[:, 1, :], xb_sb[1][:].indirect(l2[:]), ga[:, 1, :], ALU.mult)
         for t in (2, 3):
             nc.vector.tensor_tensor(prod[:, t, 0:H], xb_sb[t][:].indirect(l2[:, 0:8]), ga[:, t, 0:H], ALU.mult)
             nc.scalar.activation(gb[:, t - 2, :], xb_sb[t][:].indirect(l2[:, 8:16]), ACT.Copy)
         nc.vector.tensor_tensor(prod[:, 2:4, H:J], gb[:], ga[:, 2:4, H:J], ALU.mult)
 
-        u_bf = [sb.tile([P, H * PACK], BF16, name="u_bf%d" % h, tag="half%d" % h, align_bytes=64) for h in range(2)]
+        u_bf = [sb.tile([P, H * PACK], BF16, name="u_bf%d" % h, align_bytes=64) for h in range(2)]
         nc.scalar.copy(
             u_bf[0][:].rearrange("p (c i t) -> p c t i", i=4, t=PACK),
             prod[:, :, 0:H].rearrange("p t (c i) -> p c t i", i=4),
@@ -119,7 +112,7 @@ def tile_list_looks_entryproducts_gap_rowabove_kernel(
             nc.vector.quantize_mx(out=u_q[:, cols].bitcast(E5M2X4), scales=u_s[:, cols], in_=u_bf[h][:])
 
         g3 = sb.tile([P, PACK, O], F32, name="g3")
-        g4 = sb.tile([P, PACK, O], F32, name="g4")
+        g4 = sb.tile([P, PACK, O], F32, name="g4", tag="late")
         ha = [sb.tile([P, J], F32, name="ha%d" % t) for t in range(PACK)]
         acc = [ps.tile([P, J], F32, name="acc%d" % t) for t in range(PACK)]
 
@@ -137,8 +130,6 @@ def tile_list_looks_entryproducts_gap_rowabove_kernel(
             first_product(t, slice(0, J))
         for t in range(PACK):
             nc.scalar.activation(ha[t][:], acc[t][:], ACT.Relu)
-        nres = sb.tile([P, N], F32, name="nres", tag="half1", align_bytes=64)
-        nc.vector.tensor_scalar(nres[:], rs_sb[:], -0.3, None, ALU.mult)
         for t in range(PACK):
             if t < 3:
                 nc.vector.tensor_copy(g3[:, t, :], ha[t][:].indirect(l3[:]))
@@ -158,6 +149,8 @@ def tile_list_looks_entryproducts_gap_rowabove_kernel(
                 g4[:, pair, :].rearrange("p t (c i) -> p c t i", i=4),
                 ALU.subtract,
             )
+        nres = sb.tile([P, N], F32, name="nres", tag="late")
+        nc.scalar.activation(nres[:], rs_sb[:], ACT.Copy, scale=-0.3)
         h_q = sb.tile([P, O], U32, name="h_q", align_bytes=64)
         h_s = sb.tile([P, O], U8, name="h_s", align_bytes=64)
         nc.vector.quantize_mx(out=h_q[:].bitcast(E5M2X4), scales=h_s[:], in_=h_bf[:])
@@ -172,7 +165,7 @@ def tile_list_looks_entryproducts_gap_rowabove_kernel(
             cols = slice(h * NH, (h + 1) * NH)
             nc.tensor.matmul_mx(
                 out=pp[h][:], lhsT=h_q[:].bitcast(E5M2X4), lhsT_scale=h_s[:],
-                rhs=wb_sb[:, cols].bitcast(E4M3X4), rhs_scale=wbs[:, cols], start=True, stop=True,
+                rhs=wb_sb[:, cols].bitcast(E4M3X4), rhs_scale=ws_st[:, R + h * NH : R + (h + 1) * NH], start=True, stop=True,
             )
             nc.scalar.activation(mag[:, cols], pp[h][:], ACT.Abs, scale=1.0 / N, accum_out=mn[h][:])
         for h in range(2):

@@ -18,6 +18,21 @@ ACT = mybir.ActivationFunctionType
 
 P = 128
 PACK = 4
+ENTRIES = 16
+BLOCKS = 16
+QUADS = 4
+RUN = 4
+JH = J // 2
+NH = N // 2
+RESIDUAL = 0.3
+
+
+def side_by_side(tile):
+    return tile.rearrange("p (c i t) -> p c t i", i=RUN, t=PACK)
+
+
+def by_planes(tile):
+    return tile.rearrange("p t (c i) -> p c t i", i=RUN)
 
 
 def tile_list_looks_entryproducts_gap_rowabove_kernel(
@@ -28,150 +43,149 @@ def tile_list_looks_entryproducts_gap_rowabove_kernel(
         sb = ctx.enter_context(tc.tile_pool(name="sb", bufs=1))
         ps = ctx.enter_context(tc.psum_pool(name="ps", bufs=1))
 
-        l1 = sb.tile([P, J // 16], U16, name="l1")
-        l2 = sb.tile([P, J // 16], U16, name="l2")
-        l3 = sb.tile([P, O // 16], U16, name="l3")
-        l4 = sb.tile([P, O // 16], U16, name="l4")
+        list1 = sb.tile([P, J // ENTRIES], U16, name="list1")
+        list2 = sb.tile([P, J // ENTRIES], U16, name="list2")
+        list3 = sb.tile([P, O // ENTRIES], U16, name="list3")
+        list4 = sb.tile([P, O // ENTRIES], U16, name="list4")
         xa_sb = [sb.tile([P, 2 * T], F32, name="xa%d" % u) for u in range(2)]
         xb_sb = [sb.tile([P, S], F32, name="xb%d" % t) for t in range(PACK)]
         fk_sb = sb.tile([P, PACK], F32, name="fk_sb")
         w_raw = sb.tile([P, R], U32, name="w_raw", align_bytes=64)
         w_st = sb.tile([P, R], U32, name="w_st", align_bytes=64)
         ws_raw = sb.tile([P, R], U8, name="ws_raw", align_bytes=64)
-        ws_st = sb.tile([P, R + N], U8, name="ws_st", align_bytes=64)
+        scales = sb.tile([P, R + N], U8, name="scales", align_bytes=64)
 
         xa_rows = xa.rearrange("(p u e) c -> p u (e c)", u=2, e=2)
         xb_rows = xb.rearrange("(p t) c -> p t c", t=PACK)
 
-        warm_in = sb.tile([P, 1], F32, name="warm_in")
         warm_out = sb.tile([P, 1], F32, name="warm_out")
-        ws_mid = sb.tile([P, R + N], U8, name="ws_mid", align_bytes=64)
+        staged = sb.tile([P, R + N], U8, name="staged", align_bytes=64)
         nc.gpsimd.memset(ws_raw[:].bitcast(I32), 0)
-        nc.gpsimd.memset(warm_in[:], 0.0)
-        nc.scalar.activation(warm_out[:], warm_in[:], ACT.Abs)
-        nc.gpsimd.memset(ws_st[:].bitcast(I32), 0)
+        nc.gpsimd.memset(scales[:].bitcast(I32), 0)
+        nc.scalar.activation(warm_out[:], scales[:, 0:4].bitcast(F32), ACT.Abs)
 
-        nc.sync.dma_start(l1[:], offs)
+        nc.sync.dma_start(list1[:], offs)
         nc.sync.dma_start(fk_sb[:], fk.rearrange("(p t) one -> p (t one)", t=PACK))
         nc.sync.dma_start(xa_sb[0][:], xa_rows[:, 0, :])
-        nc.sync.dma_start(ws_mid[0:16, R : R + N].bitcast(I32), wb_scales[0].bitcast(I32))
-        nc.sync.dma_start(ws_raw[0:16, :].bitcast(I32), w_scales[0].bitcast(I32))
+        nc.sync.dma_start(staged[0:BLOCKS, R : R + N].bitcast(I32), wb_scales[0].bitcast(I32))
+        nc.sync.dma_start(ws_raw[0:BLOCKS, :].bitcast(I32), w_scales[0].bitcast(I32))
         nc.sync.dma_start(xb_sb[0][:], xb_rows[:, 0, :])
-        nc.sync.dma_start(l2[:], offs2)
+        nc.sync.dma_start(list2[:], offs2)
         nc.sync.dma_start(xa_sb[1][:], xa_rows[:, 1, :])
         for t in range(1, PACK):
             nc.sync.dma_start(xb_sb[t][:], xb_rows[:, t, :])
         nc.sync.dma_start(w_raw[:].bitcast(I32), w_words[0].rearrange("p n t -> p (n t)").bitcast(I32))
+
         nc.vector.tensor_copy(
-            ws_mid[:, 0:R].rearrange("p (t m) -> p t m", t=PACK), ws_raw[:].rearrange("p (m t) -> p t m", t=PACK)
+            staged[:, 0:R].rearrange("p (t m) -> p t m", t=PACK), ws_raw[:].rearrange("p (m t) -> p t m", t=PACK)
         )
-        for q in range(4):
-            nc.sync.dma_start(ws_st[32 * q : 32 * q + 4, :].bitcast(I32), ws_mid[4 * q : 4 * q + 4, :].bitcast(I32))
-        nc.sync.dma_start(l3[:], offs3)
-        nc.sync.dma_start(l4[:], offs4)
+        rows = BLOCKS // QUADS
+        for q in range(QUADS):
+            nc.sync.dma_start(
+                scales[32 * q : 32 * q + rows, :].bitcast(I32), staged[rows * q : rows * (q + 1), :].bitcast(I32)
+            )
+        nc.sync.dma_start(list3[:], offs3)
+        nc.sync.dma_start(list4[:], offs4)
 
-        g1 = [sb.tile([P, J], F32, name="g1_%d" % u, tag="slot%d" % u, align_bytes=64) for u in range(2)]
-        fk_rep = sb.tile([P, 2, J], F32, name="fk_rep")
-        ga = sb.tile([P, PACK, J], F32, name="ga")
-        gb = sb.tile([P, 2, J // 2], F32, name="gb")
-        prod = sb.tile([P, PACK, J], F32, name="prod")
-        H = J // 2
+        xa_odd = [sb.tile([P, J], F32, name="xa_odd%d" % u, tag="reuse%d" % u, align_bytes=64) for u in range(2)]
+        fk_even = sb.tile([P, 2, J], F32, name="fk_even")
+        xa_fk = sb.tile([P, PACK, J], F32, name="xa_fk")
+        xb_late = sb.tile([P, 2, JH], F32, name="xb_late")
+        u_f32 = sb.tile([P, PACK, J], F32, name="u_f32")
 
-        nc.vector.tensor_copy(fk_rep[:], fk_sb[:, 0:PACK:2].unsqueeze(2).to_broadcast([P, 2, J]))
+        nc.vector.tensor_copy(fk_even[:], fk_sb[:, 0:PACK:2].unsqueeze(2).to_broadcast([P, 2, J]))
         for u in range(2):
-            nc.vector.tensor_tensor(ga[:, 2 * u, :], xa_sb[u][:].indirect(l1[:]), fk_rep[:, u, :], ALU.mult)
-            nc.scalar.activation(g1[u][:], xa_sb[u][:, T : 2 * T].indirect(l1[:]), ACT.Copy)
-            nc.scalar.activation(ga[:, 2 * u + 1, :], g1[u][:], ACT.Copy, scale=fk_sb[:, 2 * u + 1 : 2 * u + 2])
-            nc.vector.tensor_tensor(prod[:, u, :], xb_sb[u][:].indirect(l2[:]), ga[:, u, :], ALU.mult)
-        wb_sb = sb.tile([P, N], U32, name="wb_sb", tag="slot0", align_bytes=64)
-        rs_sb = sb.tile([P, N], F32, name="rs_sb", tag="slot1", align_bytes=64)
+            odd = 2 * u + 1
+            nc.vector.tensor_tensor(xa_fk[:, 2 * u, :], xa_sb[u][:].indirect(list1[:]), fk_even[:, u, :], ALU.mult)
+            nc.scalar.activation(xa_odd[u][:], xa_sb[u][:, T : 2 * T].indirect(list1[:]), ACT.Copy)
+            nc.scalar.activation(xa_fk[:, odd, :], xa_odd[u][:], ACT.Copy, scale=fk_sb[:, odd : odd + 1])
+            nc.vector.tensor_tensor(u_f32[:, u, :], xb_sb[u][:].indirect(list2[:]), xa_fk[:, u, :], ALU.mult)
+
+        wb_sb = sb.tile([P, N], U32, name="wb_sb", tag="reuse0", align_bytes=64)
+        rs_sb = sb.tile([P, N], F32, name="rs_sb", tag="reuse1", align_bytes=64)
         nc.sync.dma_start(wb_sb[:].bitcast(I32), wb_words[0].rearrange("p n t -> p (n t)").bitcast(I32))
         nc.sync.dma_start(rs_sb[:], rs)
 
-        for t in (2, 3):
-            nc.vector.tensor_tensor(prod[:, t, 0:H], xb_sb[t][:].indirect(l2[:, 0:8]), ga[:, t, 0:H], ALU.mult)
-            nc.scalar.activation(gb[:, t - 2, :], xb_sb[t][:].indirect(l2[:, 8:16]), ACT.Copy)
-        nc.vector.tensor_tensor(prod[:, 2:4, H:J], gb[:], ga[:, 2:4, H:J], ALU.mult)
+        half_cols = JH // ENTRIES
+        for t in range(2, PACK):
+            nc.vector.tensor_tensor(
+                u_f32[:, t, 0:JH], xb_sb[t][:].indirect(list2[:, 0:half_cols]), xa_fk[:, t, 0:JH], ALU.mult
+            )
+            nc.scalar.activation(
+                xb_late[:, t - 2, :], xb_sb[t][:].indirect(list2[:, half_cols : 2 * half_cols]), ACT.Copy
+            )
+        nc.vector.tensor_tensor(u_f32[:, 2:PACK, JH:J], xb_late[:], xa_fk[:, 2:PACK, JH:J], ALU.mult)
 
-        u_bf = [sb.tile([P, H * PACK], BF16, name="u_bf%d" % h, align_bytes=64) for h in range(2)]
-        nc.scalar.copy(
-            u_bf[0][:].rearrange("p (c i t) -> p c t i", i=4, t=PACK),
-            prod[:, :, 0:H].rearrange("p t (c i) -> p c t i", i=4),
-        )
-        nc.vector.tensor_copy(
-            w_st[:].rearrange("p (t c i) -> p c t i", t=PACK, i=4), w_raw[:].rearrange("p (c i t) -> p c t i", i=4, t=PACK)
-        )
-        nc.vector.tensor_copy(
-            u_bf[1][:].rearrange("p (c i t) -> p c t i", i=4, t=PACK),
-            prod[:, :, H:J].rearrange("p t (c i) -> p c t i", i=4),
-        )
-        u_q = sb.tile([P, J], U32, name="u_q", align_bytes=64)
-        u_s = sb.tile([P, J], U8, name="u_s", align_bytes=64)
+        u_bf = [sb.tile([P, JH * PACK], BF16, name="u_bf%d" % h, align_bytes=64) for h in range(2)]
+        nc.scalar.copy(side_by_side(u_bf[0][:]), by_planes(u_f32[:, :, 0:JH]))
+        nc.vector.tensor_copy(w_st[:].rearrange("p (t c i) -> p c t i", t=PACK, i=RUN), side_by_side(w_raw[:]))
+        nc.vector.tensor_copy(side_by_side(u_bf[1][:]), by_planes(u_f32[:, :, JH:J]))
+        u_codes = sb.tile([P, J], U32, name="u_codes", align_bytes=64)
+        u_scales = sb.tile([P, J], U8, name="u_scales", align_bytes=64)
         for h in range(2):
-            cols = slice(h * H, (h + 1) * H)
-            nc.vector.quantize_mx(out=u_q[:, cols].bitcast(E5M2X4), scales=u_s[:, cols], in_=u_bf[h][:])
+            slots = slice(h * JH, (h + 1) * JH)
+            nc.vector.quantize_mx(out=u_codes[:, slots].bitcast(E5M2X4), scales=u_scales[:, slots], in_=u_bf[h][:])
 
-        g3 = sb.tile([P, PACK, O], F32, name="g3")
-        g4 = sb.tile([P, PACK, O], F32, name="g4", tag="late")
+        ha_by3 = sb.tile([P, PACK, O], F32, name="ha_by3")
+        ha_by4 = sb.tile([P, PACK, O], F32, name="ha_by4", tag="reuse2")
         ha = [sb.tile([P, J], F32, name="ha%d" % t) for t in range(PACK)]
-        acc = [ps.tile([P, J], F32, name="acc%d" % t) for t in range(PACK)]
+        a_ps = [ps.tile([P, J], F32, name="a_ps%d" % t) for t in range(PACK)]
 
         def first_product(t, slots):
             cols = slice(t * P, (t + 1) * P)
             nc.tensor.matmul_mx(
-                out=acc[t][:, slots], lhsT=w_st[:, cols].bitcast(E5M2X4), lhsT_scale=ws_st[:, cols],
-                rhs=u_q[:, slots].bitcast(E5M2X4), rhs_scale=u_s[:, slots], start=True, stop=True,
+                out=a_ps[t][:, slots], lhsT=w_st[:, cols].bitcast(E5M2X4), lhsT_scale=scales[:, cols],
+                rhs=u_codes[:, slots].bitcast(E5M2X4), rhs_scale=u_scales[:, slots], start=True, stop=True,
             )
 
         for h in range(2):
             for t in range(2):
-                first_product(t, slice(h * H, (h + 1) * H))
+                first_product(t, slice(h * JH, (h + 1) * JH))
         for t in range(2, PACK):
             first_product(t, slice(0, J))
         for t in range(PACK):
-            nc.scalar.activation(ha[t][:], acc[t][:], ACT.Relu)
-        for t in range(PACK):
-            if t < 3:
-                nc.vector.tensor_copy(g3[:, t, :], ha[t][:].indirect(l3[:]))
-            else:
-                nc.scalar.activation(g3[:, t, :], ha[t][:].indirect(l3[:]), ACT.Copy)
-            if t < 2:
-                nc.vector.tensor_copy(g4[:, t, :], ha[t][:].indirect(l4[:]))
-            else:
-                nc.scalar.activation(g4[:, t, :], ha[t][:].indirect(l4[:]), ACT.Copy)
+            nc.scalar.activation(ha[t][:], a_ps[t][:], ACT.Relu)
 
-        h_bf = sb.tile([P, O * PACK], BF16, name="h_bf", align_bytes=64)
+        on_vector = 5
+        for t in range(PACK):
+            for e, (picked, entries) in enumerate(((ha_by3, list3), (ha_by4, list4))):
+                if 2 * t + e < on_vector:
+                    nc.vector.tensor_copy(picked[:, t, :], ha[t][:].indirect(entries[:]))
+                else:
+                    nc.scalar.activation(picked[:, t, :], ha[t][:].indirect(entries[:]), ACT.Copy)
+
+        hid_bf = sb.tile([P, O * PACK], BF16, name="hid_bf", align_bytes=64)
         for u in range(2):
             pair = slice(2 * u, 2 * u + 2)
             nc.vector.tensor_tensor(
-                h_bf[:].rearrange("p (c i t) -> p c t i", i=4, t=PACK)[:, :, pair, :],
-                g3[:, pair, :].rearrange("p t (c i) -> p c t i", i=4),
-                g4[:, pair, :].rearrange("p t (c i) -> p c t i", i=4),
+                side_by_side(hid_bf[:])[:, :, pair, :], by_planes(ha_by3[:, pair, :]), by_planes(ha_by4[:, pair, :]),
                 ALU.subtract,
             )
-        nres = sb.tile([P, N], F32, name="nres", tag="late")
-        nc.scalar.activation(nres[:], rs_sb[:], ACT.Copy, scale=-0.3)
-        h_q = sb.tile([P, O], U32, name="h_q", align_bytes=64)
-        h_s = sb.tile([P, O], U8, name="h_s", align_bytes=64)
-        nc.vector.quantize_mx(out=h_q[:].bitcast(E5M2X4), scales=h_s[:], in_=h_bf[:])
+        neg_res = sb.tile([P, N], F32, name="neg_res", tag="reuse2")
+        nc.scalar.activation(neg_res[:], rs_sb[:], ACT.Copy, scale=-RESIDUAL)
+        hid_codes = sb.tile([P, O], U32, name="hid_codes", align_bytes=64)
+        hid_scales = sb.tile([P, O], U8, name="hid_scales", align_bytes=64)
+        nc.vector.quantize_mx(out=hid_codes[:].bitcast(E5M2X4), scales=hid_scales[:], in_=hid_bf[:])
 
-        NH = N // 2
-        pp = [ps.tile([P, NH], F32, name="pp%d" % h) for h in range(2)]
+        p_ps = [ps.tile([P, NH], F32, name="p_ps%d" % h) for h in range(2)]
         mag = sb.tile([P, N], F32, name="mag")
-        mn = [sb.tile([P, 1], F32, name="mn%d" % h) for h in range(2)]
-        qq = sb.tile([P, N], F32, name="qq")
+        part = [sb.tile([P, 1], F32, name="part%d" % h) for h in range(2)]
+        shifted = sb.tile([P, N], F32, name="shifted")
         y = sb.tile([P, N], F32, name="y")
-        for h in range(2):
-            cols = slice(h * NH, (h + 1) * NH)
+        halves = [slice(h * NH, (h + 1) * NH) for h in range(2)]
+        for h, cols in enumerate(halves):
             nc.tensor.matmul_mx(
-                out=pp[h][:], lhsT=h_q[:].bitcast(E5M2X4), lhsT_scale=h_s[:],
-                rhs=wb_sb[:, cols].bitcast(E4M3X4), rhs_scale=ws_st[:, R + h * NH : R + (h + 1) * NH], start=True, stop=True,
+                out=p_ps[h][:], lhsT=hid_codes[:].bitcast(E5M2X4), lhsT_scale=hid_scales[:],
+                rhs=wb_sb[:, cols].bitcast(E4M3X4), rhs_scale=scales[:, R + cols.start : R + cols.stop],
+                start=True, stop=True,
             )
-            nc.scalar.activation(mag[:, cols], pp[h][:], ACT.Abs, scale=1.0 / N, accum_out=mn[h][:])
-        for h in range(2):
-            cols = slice(h * NH, (h + 1) * NH)
-            nc.vector.scalar_tensor_tensor(qq[:, cols], pp[h][:], mn[0][:], nres[:, cols], ALU.subtract, ALU.add)
-        for h in range(2):
-            cols = slice(h * NH, (h + 1) * NH)
-            nc.vector.scalar_tensor_tensor(y[:, cols], qq[:, cols], mn[1][:], nres[:, cols], ALU.subtract, ALU.max)
-        nc.sync.dma_start(out, y[:])
+            nc.scalar.activation(mag[:, cols], p_ps[h][:], ACT.Abs, scale=1.0 / N, accum_out=part[h][:])
+        for h, cols in enumerate(halves):
+            nc.vector.scalar_tensor_tensor(
+                shifted[:, cols], p_ps[h][:], part[0][:], neg_res[:, cols], ALU.subtract, ALU.add
+            )
+        for cols in halves:
+            nc.vector.scalar_tensor_tensor(
+                y[:, cols], shifted[:, cols], part[1][:], neg_res[:, cols], ALU.subtract, ALU.max
+            )
+            nc.sync.dma_start(out[:, cols], y[:, cols])

from contextlib import ExitStack

import concourse.mybir as mybir

K, T, J, S, R, O, N = 512, 512, 256, 512, 512, 128, 256
FLOPS = 2 * K * R * J + 2 * R * O * N

F32 = mybir.dt.float32
BF16 = mybir.dt.bfloat16
I32 = mybir.dt.int32
U32 = mybir.dt.uint32
U16 = mybir.dt.uint16
U8 = mybir.dt.uint8
E5M2X4 = mybir.dt.float8_e5m2_x4
E4M3X4 = mybir.dt.float8_e4m3fn_x4
ALU = mybir.AluOpType
ACT = mybir.ActivationFunctionType

P = 128
PACK = 4
ENTRIES = 16
BLOCKS = 16
QUADS = 4
RUN = 4
JH = J // 2
NH = N // 2
RESIDUAL = 0.3


def side_by_side(tile):
    return tile.rearrange("p (c i t) -> p c t i", i=RUN, t=PACK)


def by_planes(tile):
    return tile.rearrange("p t (c i) -> p c t i", i=RUN)


def tile_list_looks_entryproducts_gap_rowabove_kernel(
    tc, xa, xb, fk, w_words, w_scales, wb_words, wb_scales, rs, offs, offs2, offs3, offs4, out
):
    nc = tc.nc
    with ExitStack() as ctx:
        sb = ctx.enter_context(tc.tile_pool(name="sb", bufs=1))
        ps = ctx.enter_context(tc.psum_pool(name="ps", bufs=1))

        list1 = sb.tile([P, J // ENTRIES], U16, name="list1")
        list2 = sb.tile([P, J // ENTRIES], U16, name="list2")
        list3 = sb.tile([P, O // ENTRIES], U16, name="list3")
        list4 = sb.tile([P, O // ENTRIES], U16, name="list4")
        xa_sb = [sb.tile([P, 2 * T], F32, name="xa%d" % u) for u in range(2)]
        xb_sb = [sb.tile([P, S], F32, name="xb%d" % t) for t in range(PACK)]
        fk_sb = sb.tile([P, PACK], F32, name="fk_sb")
        w_raw = sb.tile([P, R], U32, name="w_raw", align_bytes=64)
        w_st = sb.tile([P, R], U32, name="w_st", align_bytes=64)
        ws_raw = sb.tile([P, R], U8, name="ws_raw", align_bytes=64)
        scales = sb.tile([P, R + N], U8, name="scales", align_bytes=64)

        xa_rows = xa.rearrange("(p u e) c -> p u (e c)", u=2, e=2)
        xb_rows = xb.rearrange("(p t) c -> p t c", t=PACK)

        warm_out = sb.tile([P, 1], F32, name="warm_out")
        staged = sb.tile([P, R + N], U8, name="staged", align_bytes=64)
        nc.gpsimd.memset(ws_raw[:].bitcast(I32), 0)
        nc.gpsimd.memset(scales[:].bitcast(I32), 0)
        nc.scalar.activation(warm_out[:], scales[:, 0:4].bitcast(F32), ACT.Abs)

        nc.sync.dma_start(list1[:], offs)
        nc.sync.dma_start(fk_sb[:], fk.rearrange("(p t) one -> p (t one)", t=PACK))
        nc.sync.dma_start(xa_sb[0][:], xa_rows[:, 0, :])
        nc.sync.dma_start(staged[0:BLOCKS, R : R + N].bitcast(I32), wb_scales[0].bitcast(I32))
        nc.sync.dma_start(ws_raw[0:BLOCKS, :].bitcast(I32), w_scales[0].bitcast(I32))
        nc.sync.dma_start(xb_sb[0][:], xb_rows[:, 0, :])
        nc.sync.dma_start(list2[:], offs2)
        nc.sync.dma_start(xa_sb[1][:], xa_rows[:, 1, :])
        for t in range(1, PACK):
            nc.sync.dma_start(xb_sb[t][:], xb_rows[:, t, :])
        nc.sync.dma_start(w_raw[:].bitcast(I32), w_words[0].rearrange("p n t -> p (n t)").bitcast(I32))

        nc.vector.tensor_copy(
            staged[:, 0:R].rearrange("p (t m) -> p t m", t=PACK), ws_raw[:].rearrange("p (m t) -> p t m", t=PACK)
        )
        rows = BLOCKS // QUADS
        for q in range(QUADS):
            nc.sync.dma_start(
                scales[32 * q : 32 * q + rows, :].bitcast(I32), staged[rows * q : rows * (q + 1), :].bitcast(I32)
            )
        nc.sync.dma_start(list3[:], offs3)
        nc.sync.dma_start(list4[:], offs4)

        xa_odd = [sb.tile([P, J], F32, name="xa_odd%d" % u, tag="reuse%d" % u, align_bytes=64) for u in range(2)]
        fk_even = sb.tile([P, 2, J], F32, name="fk_even")
        xa_fk = sb.tile([P, PACK, J], F32, name="xa_fk")
        xb_late = sb.tile([P, 2, JH], F32, name="xb_late")
        u_f32 = sb.tile([P, PACK, J], F32, name="u_f32")

        nc.vector.tensor_copy(fk_even[:], fk_sb[:, 0:PACK:2].unsqueeze(2).to_broadcast([P, 2, J]))
        for u in range(2):
            odd = 2 * u + 1
            nc.vector.tensor_tensor(xa_fk[:, 2 * u, :], xa_sb[u][:].indirect(list1[:]), fk_even[:, u, :], ALU.mult)
            nc.scalar.activation(xa_odd[u][:], xa_sb[u][:, T : 2 * T].indirect(list1[:]), ACT.Copy)
            nc.scalar.activation(xa_fk[:, odd, :], xa_odd[u][:], ACT.Copy, scale=fk_sb[:, odd : odd + 1])
            nc.vector.tensor_tensor(u_f32[:, u, :], xb_sb[u][:].indirect(list2[:]), xa_fk[:, u, :], ALU.mult)

        wb_sb = sb.tile([P, N], U32, name="wb_sb", tag="reuse0", align_bytes=64)
        rs_sb = sb.tile([P, N], F32, name="rs_sb", tag="reuse1", align_bytes=64)
        nc.sync.dma_start(wb_sb[:].bitcast(I32), wb_words[0].rearrange("p n t -> p (n t)").bitcast(I32))
        nc.sync.dma_start(rs_sb[:], rs)

        half_cols = JH // ENTRIES
        for t in range(2, PACK):
            nc.vector.tensor_tensor(
                u_f32[:, t, 0:JH], xb_sb[t][:].indirect(list2[:, 0:half_cols]), xa_fk[:, t, 0:JH], ALU.mult
            )
            nc.scalar.activation(
                xb_late[:, t - 2, :], xb_sb[t][:].indirect(list2[:, half_cols : 2 * half_cols]), ACT.Copy
            )
        nc.vector.tensor_tensor(u_f32[:, 2:PACK, JH:J], xb_late[:], xa_fk[:, 2:PACK, JH:J], ALU.mult)

        u_bf = [sb.tile([P, JH * PACK], BF16, name="u_bf%d" % h, align_bytes=64) for h in range(2)]
        nc.scalar.copy(side_by_side(u_bf[0][:]), by_planes(u_f32[:, :, 0:JH]))
        nc.vector.tensor_copy(w_st[:].rearrange("p (t c i) -> p c t i", t=PACK, i=RUN), side_by_side(w_raw[:]))
        nc.vector.tensor_copy(side_by_side(u_bf[1][:]), by_planes(u_f32[:, :, JH:J]))
        u_codes = sb.tile([P, J], U32, name="u_codes", align_bytes=64)
        u_scales = sb.tile([P, J], U8, name="u_scales", align_bytes=64)
        for h in range(2):
            slots = slice(h * JH, (h + 1) * JH)
            nc.vector.quantize_mx(out=u_codes[:, slots].bitcast(E5M2X4), scales=u_scales[:, slots], in_=u_bf[h][:])

        ha_by3 = sb.tile([P, PACK, O], F32, name="ha_by3")
        ha_by4 = sb.tile([P, PACK, O], F32, name="ha_by4", tag="reuse2")
        ha = [sb.tile([P, J], F32, name="ha%d" % t) for t in range(PACK)]
        a_ps = [ps.tile([P, J], F32, name="a_ps%d" % t) for t in range(PACK)]

        def first_product(t, slots):
            cols = slice(t * P, (t + 1) * P)
            nc.tensor.matmul_mx(
                out=a_ps[t][:, slots], lhsT=w_st[:, cols].bitcast(E5M2X4), lhsT_scale=scales[:, cols],
                rhs=u_codes[:, slots].bitcast(E5M2X4), rhs_scale=u_scales[:, slots], start=True, stop=True,
            )

        for h in range(2):
            for t in range(2):
                first_product(t, slice(h * JH, (h + 1) * JH))
        for t in range(2, PACK):
            first_product(t, slice(0, J))
        for t in range(PACK):
            nc.scalar.activation(ha[t][:], a_ps[t][:], ACT.Relu)

        on_vector = 5
        for t in range(PACK):
            for e, (picked, entries) in enumerate(((ha_by3, list3), (ha_by4, list4))):
                if 2 * t + e < on_vector:
                    nc.vector.tensor_copy(picked[:, t, :], ha[t][:].indirect(entries[:]))
                else:
                    nc.scalar.activation(picked[:, t, :], ha[t][:].indirect(entries[:]), ACT.Copy)

        hid_bf = sb.tile([P, O * PACK], BF16, name="hid_bf", align_bytes=64)
        for u in range(2):
            pair = slice(2 * u, 2 * u + 2)
            nc.vector.tensor_tensor(
                side_by_side(hid_bf[:])[:, :, pair, :], by_planes(ha_by3[:, pair, :]), by_planes(ha_by4[:, pair, :]),
                ALU.subtract,
            )
        neg_res = sb.tile([P, N], F32, name="neg_res", tag="reuse2")
        nc.scalar.activation(neg_res[:], rs_sb[:], ACT.Copy, scale=-RESIDUAL)
        hid_codes = sb.tile([P, O], U32, name="hid_codes", align_bytes=64)
        hid_scales = sb.tile([P, O], U8, name="hid_scales", align_bytes=64)
        nc.vector.quantize_mx(out=hid_codes[:].bitcast(E5M2X4), scales=hid_scales[:], in_=hid_bf[:])

        p_ps = [ps.tile([P, NH], F32, name="p_ps%d" % h) for h in range(2)]
        mag = sb.tile([P, N], F32, name="mag")
        part = [sb.tile([P, 1], F32, name="part%d" % h) for h in range(2)]
        shifted = sb.tile([P, N], F32, name="shifted")
        y = sb.tile([P, N], F32, name="y")
        halves = [slice(h * NH, (h + 1) * NH) for h in range(2)]
        for h, cols in enumerate(halves):
            nc.tensor.matmul_mx(
                out=p_ps[h][:], lhsT=hid_codes[:].bitcast(E5M2X4), lhsT_scale=hid_scales[:],
                rhs=wb_sb[:, cols].bitcast(E4M3X4), rhs_scale=scales[:, R + cols.start : R + cols.stop],
                start=True, stop=True,
            )
            nc.scalar.activation(mag[:, cols], p_ps[h][:], ACT.Abs, scale=1.0 / N, accum_out=part[h][:])
        for h, cols in enumerate(halves):
            nc.vector.scalar_tensor_tensor(
                shifted[:, cols], p_ps[h][:], part[0][:], neg_res[:, cols], ALU.subtract, ALU.add
            )
        for cols in halves:
            nc.vector.scalar_tensor_tensor(
                y[:, cols], shifted[:, cols], part[1][:], neg_res[:, cols], ALU.subtract, ALU.max
            )
            nc.sync.dma_start(out[:, cols], y[:, cols])
